import numpy as np
import ml_dtypes


def mxq(x, axis, fmt="e4m3"):
    dtype, down = {"e4m3": (ml_dtypes.float8_e4m3fn, 7), "e5m2": (ml_dtypes.float8_e5m2, 14)}[fmt]
    v = np.moveaxis(np.asarray(x, np.float32).astype(ml_dtypes.bfloat16).astype(np.float64), axis, -1)
    blocks = v.reshape(v.shape[:-1] + (-1, 32))
    amax = np.abs(blocks).max(-1, keepdims=True)
    byte = np.maximum(np.where(amax > 0, np.frexp(amax)[1] - 1 + 127, 0) - down, 1)
    scale = np.exp2(byte - 127.0)
    codes = (blocks / scale).astype(np.float32).astype(dtype).astype(np.float64)
    return np.moveaxis((codes * scale).reshape(v.shape), -1, axis)


WIDE = False


def mx_kscale(k):
    if not WIDE:
        return np.ones(k)
    levels = np.array([10, -10, 5, -5, 0])
    if k % 512:
        return np.exp2(np.random.permutation(np.resize(levels, k // 32))).repeat(32)
    a = np.empty((k // 512, 16))
    for p in range(k // 512):
        a[p, :8] = np.random.permutation(np.resize(levels, 8))
        for g in range(8):
            far = levels[np.abs(levels - a[p, g]) >= 10]
            a[p, g + 8] = far[np.random.randint(len(far))]
    return np.exp2(a.ravel()).repeat(32)


BF16 = ml_dtypes.bfloat16


def bf(x):
    return np.asarray(x, np.float32).astype(BF16)


def f64(x):
    return np.asarray(x).astype(np.float64)


T, D, N = 2048, 1024, 1024


def setup_inputs():
    s, u = mx_kscale(D), mx_kscale(T)
    return {"keys": bf(np.random.standard_normal((T, D)) * np.exp(0.3 * np.random.standard_normal((T, 1)))),
            "values": bf(np.random.standard_normal((T, N))),
            "memory": bf(np.random.standard_normal((D, N)) / s[:, None]),
            "momentum": bf(0.5 * np.random.standard_normal((D, N))),
            "read_gain": bf((1.0 + 0.1 * np.random.standard_normal(D)) * s),
            "write_gain": bf(1.0 + 0.1 * np.random.standard_normal(D)),
            "beta": bf(np.random.uniform(0.2, 0.8, T) * u),
            "hold": bf(np.random.uniform(0.3, 0.9, T) / u),
            "decay": bf(np.random.uniform(0.8, 1.0, D) * s),
            "mu": bf(np.random.uniform(0.5, 0.9, D))}


def reference(keys, values, memory, momentum, read_gain, write_gain, beta, hold, decay, mu):
    k = f64(keys)
    m = f64(memory)
    kn = k / np.sqrt(np.sum(k * k, axis=1, keepdims=True))
    kr = kn * f64(read_gain)[None, :]
    kw = kn * f64(write_gain)[None, :] * f64(hold)[:, None]
    pred = mxq(kr, 1, "e4m3") @ mxq(m, 0, "e4m3")
    err = f64(beta)[:, None] * (f64(values) - pred)
    upd = mxq(kw, 0, "e4m3").T @ mxq(err, 0, "e4m3")
    new_momentum = f64(mu)[:, None] * f64(momentum) + upd
    new_memory = f64(decay)[:, None] * m + new_momentum
    return new_memory, new_momentum

@@ -1,0 +1,393 @@
+from contextlib import ExitStack
+
+import concourse.mybir as mybir
+from concourse.masks import make_identity
+
+F32 = mybir.dt.float32
+BF16 = mybir.dt.bfloat16
+U32 = mybir.dt.uint32
+U8 = mybir.dt.uint8
+FP8X4 = mybir.dt.float8_e4m3fn_x4
+ACT = mybir.ActivationFunctionType
+ALU = mybir.AluOpType
+
+P = 128
+T, D, N = 2048, 1024, 1024
+PACK = 4
+GROUPS = T // 512
+HALVES = D // 512
+NH = 512
+TABLE_HALVES = (0,)
+POOL_HALVES = (1,)
+EARLY = 2
+RUN = 4
+
+FLOPS = 2 * 2 * T * D * N
+
+
+def tile_delta_memory_chunk_f4_kernel(
+    tc, keys, values, memory, momentum, read_gain, write_gain, beta, hold, decay, mu, new_memory, new_momentum
+):
+    nc = tc.nc
+    with ExitStack() as ctx:
+        const = ctx.enter_context(tc.tile_pool(name="const", bufs=1))
+        raw = ctx.enter_context(tc.tile_pool(name="raw", bufs=7))
+        work = ctx.enter_context(tc.tile_pool(name="work", bufs=2))
+        stats = ctx.enter_context(tc.tile_pool(name="stats", bufs=4))
+        psc = ctx.enter_context(tc.psum_pool(name="psc", bufs=1))
+        psum = ctx.enter_context(tc.psum_pool(name="psum", bufs=2))
+
+        vec_rows = const.tile([P, P], BF16)
+        tok_rows = const.tile([P, 512], BF16)
+        nc.vector.memset(vec_rows[:], 0.0)
+        nc.vector.memset(tok_rows[:], 0.0)
+        table = const.tile([P, 4, PACK, P], BF16)
+        nc.gpsimd.memset(table[:], 0.0)
+        for i, vec in enumerate((read_gain, write_gain, mu, decay)):
+            nc.scalar.dma_start(out=vec_rows[8 * i : 8 * i + 8, :], in_=vec.rearrange("(r c) -> r c", c=P))
+        nc.scalar.dma_start(out=tok_rows[0:4, :], in_=beta.rearrange("(g c) -> g c", c=512))
+        nc.scalar.dma_start(out=tok_rows[4:8, :], in_=hold.rearrange("(g c) -> g c", c=512))
+
+        def new_raw(name):
+            t = raw.tile([P, PACK, 1024], BF16, name=name, tag="raw")
+            return t
+
+        key_t, val_t, mem_t = [], [], {}
+        k0 = new_raw("k0")
+
+        def load_k0(j):
+            nc.sync.dma_start(
+                out=k0[:, j, :], in_=keys[0:512, :].rearrange("(p j) d -> p j d", j=PACK)[:, j, :]
+            )
+
+        def load_mem(h, nh):
+            cols = slice(nh * NH, (nh + 1) * NH)
+            t = raw.tile([P, PACK, NH], BF16, name="m%d%d" % (h, nh), tag="mraw", bufs=4)
+            nc.sync.dma_start(
+                out=t[:], in_=memory[h * 512 : (h + 1) * 512, cols].rearrange("(p j) n -> p j n", j=PACK)
+            )
+            mem_t[h, nh] = t
+
+        load_k0(0)
+        load_k0(1)
+        load_mem(0, 0)
+        load_k0(2)
+        load_k0(3)
+        load_mem(1, 0)
+        key_t.append(k0)
+
+        def load4(src, r0, name):
+            t = new_raw(name)
+            nc.sync.dma_start(out=t[:], in_=src[r0 : r0 + 512, :].rearrange("(p j) d -> p j d", j=PACK))
+            return t
+
+        key_t.append(load4(keys, 512, "k1"))
+        load_mem(0, 1)
+        load_mem(1, 1)
+        val_t.append(load4(values, 0, "v0"))
+        key_t.append(load4(keys, 1024, "k2"))
+        val_t.append(load4(values, 512, "v1"))
+        key_t.append(load4(keys, 1536, "k3"))
+        val_t.append(load4(values, 1024, "v2"))
+
+        ident = const.tile([P, P], BF16)
+        make_identity(nc, ident[:])
+        ident_f32 = const.tile([P, P], F32)
+        make_identity(nc, ident_f32[:])
+        mhalf = const.tile([P, PACK], F32)
+        nc.gpsimd.memset(mhalf[:], -0.5)
+
+        for j in range(PACK):
+            nc.scalar.dma_start(
+                out=table[j : 12 : PACK, :, j, :],
+                in_=write_gain[0:512].rearrange("(o c m) -> o c m", o=1, m=P).to_broadcast([3, 4, P]),
+            )
+
+        vec_ps = psum.tile([P, P], BF16, name="vec_ps", tag="aux")
+        nc.tensor.transpose(vec_ps[:], vec_rows[:], ident[:])
+        gain_cols = const.tile([P, 16], BF16)
+        nc.scalar.copy(gain_cols[:], vec_ps[:, 0:16])
+        rate_cols = const.tile([P, 16], F32)
+        nc.scalar.copy(rate_cols[:], vec_ps[:, 16:32])
+
+        rg_ps = psc.tile([P, D], BF16)
+        for r in range(8):
+            nc.tensor.transpose(
+                rg_ps[:, r * P : (r + 1) * P], gain_cols[:, r : r + 1].to_broadcast([P, P]), ident[:]
+            )
+        wg_ps = psum.tile([P, D], BF16, name="wg_ps", tag="aux")
+        for r in range(8):
+            nc.tensor.transpose(
+                wg_ps[:, r * P : (r + 1) * P], gain_cols[:, 8 + r : 9 + r].to_broadcast([P, P]), ident[:]
+            )
+        wgb = const.tile([P, D], BF16)
+        nc.scalar.copy(wgb[:], wg_ps[:])
+
+        tok_ps = psum.tile([P, PACK, P], BF16, name="tok_ps", tag="aux")
+        for j in range(PACK):
+            nc.tensor.transpose(tok_ps[:, j, :], tok_rows[:, j:512:PACK], ident[:])
+        tokv = const.tile([P, 8, PACK], F32)
+        nc.scalar.copy(tokv[:], tok_ps[:, :, 0:8].rearrange("p j k -> p k j"))
+
+        bdiag = const.tile([P, 16, P], BF16)
+        nc.gpsimd.tensor_tensor(
+            out=bdiag[:],
+            in0=ident[:].unsqueeze(1).to_broadcast([P, 16, P]),
+            in1=tokv[:, 0:4, :].rearrange("p g j -> p (g j)").unsqueeze(2).to_broadcast([P, 16, P]),
+            op=ALU.mult,
+        )
+
+        def plane(name, cols):
+            codes = const.tile([P, cols], U32, name=name + "_c", align_bytes=64)
+            scales = const.tile([P, cols], U8, name=name + "_s", align_bytes=64)
+            return codes, scales
+
+        mq = [plane("mq0", N), plane("mq1", N)]
+        krq = {}
+        kwq = [plane("kwq0", D), plane("kwq1", D), plane("kwq2", D), plane("kwq3", D)]
+        erq = [plane("erq0", N), plane("erq1", N), plane("erq2", N), plane("erq3", N)]
+
+        def quantize(dst, c0, src):
+            width = src.shape[-1] // PACK
+            nc.vector.quantize_mx(
+                out=dst[0][:, c0 : c0 + width].bitcast(FP8X4), scales=dst[1][:, c0 : c0 + width], in_=src
+            )
+
+        def mem_quant(h, nh):
+            mi = work.tile([P, NH, PACK], BF16, name="mi", tag="i4k", bufs=4, align_bytes=64)
+            src = mem_t[h, nh][:]
+            nc.vector.tensor_copy(
+                out=mi[:].rearrange("p (c i) j -> p c j i", i=RUN),
+                in_=src.rearrange("p j (c i) -> p c j i", i=RUN),
+            )
+            quantize(mq[h], nh * NH, mi[:].rearrange("p n j -> p (n j)"))
+
+        rs_t, hs_t = {}, {}
+
+        def prep(g):
+            ss = stats.tile([P, PACK], F32, name="ss", tag="ss")
+            for j in range(PACK):
+                sq = work.tile([P, D], BF16, name="sq", tag="sq", bufs=1)
+                nc.scalar.activation(out=sq[:], in_=key_t[g][:, j, :], func=ACT.Square, accum_out=ss[:, j : j + 1])
+            rs = stats.tile([P, PACK], F32, name="rs", tag="rs")
+            nc.gpsimd.tensor_tensor(out=rs[:], in0=ss[:], in1=mhalf[:], op=ALU.pow)
+            hs = stats.tile([P, PACK], F32, name="hs", tag="hs")
+            nc.gpsimd.tensor_tensor(out=hs[:], in0=rs[:], in1=tokv[:, 4 + g, :], op=ALU.mult)
+            rs_t[g], hs_t[g] = rs, hs
+
+        def kr(g):
+            codes = raw.tile([P, 1024], U32, name="krq_c%d" % g, tag="krq_c", bufs=3, align_bytes=64)
+            scales = raw.tile([P, 1024], U8, name="krq_s%d" % g, tag="krq_s", bufs=3, align_bytes=64)
+            krq[g] = (codes, scales)
+            for jp in range(2):
+                ki = work.tile([P, 2, 2, P, PACK], BF16, name="ki", tag="i4k", bufs=4, align_bytes=64)
+                for j2 in range(2):
+                    j = 2 * jp + j2
+                    kb = work.tile([P, D], BF16, name="kb", tag="kb", bufs=3)
+                    nc.vector.scalar_tensor_tensor(
+                        out=kb[:],
+                        in0=key_t[g][:, j, :],
+                        scalar=rs_t[g][:, j : j + 1],
+                        in1=rg_ps[:],
+                        op0=ALU.mult,
+                        op1=ALU.mult,
+                    )
+                    words = kb[:].bitcast(F32)
+                    tp = psum.tile([P, 2, 2, P], F32, name="tp", tag="tu", bufs=3)
+                    for h in range(2):
+                        for u in range(2):
+                            nc.tensor.transpose(
+                                tp[:, h, u, :], words[:, 256 * h + u : 256 * (h + 1) : 2], ident_f32[:]
+                            )
+                    dst = ki[:].rearrange("p h j m t -> p (h j m t)").bitcast(F32)
+                    dst = dst.rearrange("p (h j m u) -> p h j m u", h=2, j=2, u=2)
+                    nc.scalar.copy(dst[:, :, j2, :, :], tp[:].rearrange("p h u m -> p h m u"))
+                quantize(krq[g], 512 * jp, ki[:].rearrange("p h j m t -> p (h j m t)"))
+
+        def kw_table(g):
+            st = stats.tile([P, P], BF16, name="st%d" % g, tag="st%d" % g, bufs=1)
+            nc.gpsimd.memset(st[:], 0.0)
+            hs = hs_t[g]
+            r1 = stats.tile([P, PACK], F32, name="r1", tag="r1", bufs=2)
+            r2 = stats.tile([P, PACK], F32, name="r2", tag="r2", bufs=2)
+            nc.gpsimd.tensor_copy(out=st[:, 0:4], in_=hs[:])
+            nc.gpsimd.tensor_tensor(out=r1[:], in0=hs[:], in1=st[:, 0:4], op=ALU.subtract)
+            nc.gpsimd.tensor_copy(out=st[:, 4:8], in_=r1[:])
+            nc.gpsimd.tensor_tensor(out=r2[:], in0=r1[:], in1=st[:, 4:8], op=ALU.subtract)
+            nc.gpsimd.tensor_copy(out=st[:, 8:12], in_=r2[:])
+            hp = psum.tile([P, P], BF16, name="hp", tag="aux")
+            nc.tensor.transpose(hp[:], st[:], ident[:])
+            ht = stats.tile([P, P], BF16, name="ht", tag="ht", bufs=2)
+            nc.scalar.copy(ht[:], hp[:])
+            for half in TABLE_HALVES:
+                wi = work.tile([P, NH, PACK], BF16, name="wi", tag="i4k", bufs=4, align_bytes=64)
+                for q in range(4):
+                    c = 4 * half + q
+                    fb = psum.tile([P, 512], F32, name="fb", tag="aux")
+                    nc.tensor.matmul(
+                        fb[:], lhsT=ht[:], rhs=table[:, c, :, :].rearrange("p j m -> p (j m)"), start=True, stop=True
+                    )
+                    nc.vector.tensor_tensor(
+                        out=wi[:, q * P : (q + 1) * P, :].rearrange("p (c i) j -> p c j i", i=RUN),
+                        in0=key_t[g][:, :, c * P : (c + 1) * P].rearrange("p j (c i) -> p c j i", i=RUN),
+                        in1=fb[:].rearrange("p (j c i) -> p c j i", j=PACK, i=RUN),
+                        op=ALU.mult,
+                    )
+                quantize(kwq[g], half * 512, wi[:].rearrange("p n j -> p (n j)"))
+
+        def kw_pool(g):
+            for half in POOL_HALVES:
+                ks = work.tile([P, PACK, NH], F32, name="ks", tag="ks", bufs=1)
+                for j in range(PACK):
+                    nc.scalar.activation(
+                        out=ks[:, j, :],
+                        in_=key_t[g][:, j, half * NH : (half + 1) * NH],
+                        func=ACT.Copy,
+                        scale=hs_t[g][:, j : j + 1],
+                    )
+                wi = work.tile([P, NH, PACK], BF16, name="wg", tag="g4k", bufs=2, align_bytes=64)
+                for q in range(4):
+                    cols = slice(q * P, (q + 1) * P)
+                    gains = wgb[:, half * NH + q * P : half * NH + (q + 1) * P]
+                    nc.gpsimd.tensor_tensor(
+                        out=wi[:, cols, :],
+                        in0=ks[:, :, cols].rearrange("p j d -> p d j"),
+                        in1=gains.unsqueeze(2).to_broadcast([P, P, PACK]),
+                        op=ALU.mult,
+                    )
+                quantize(kwq[g], half * 512, wi[:].rearrange("p n j -> p (n j)"))
+
+        def kw(g):
+            kw_table(g)
+            kw_pool(g)
+
+        def err(g, nh):
+            bp = work.tile([P, PACK, NH], F32, name="bp", tag="bp", bufs=2)
+            for j in range(PACK):
+                pp = psum.tile([P, NH], F32, name="pp", tag="pp")
+                for h in range(HALVES):
+                    col = (((j // 2) * 2 + h) * 2 + j % 2) * P
+                    nc.tensor.matmul_mx(
+                        out=pp[:],
+                        lhsT=krq[g][0][:, col : col + P].bitcast(FP8X4),
+                        lhsT_scale=krq[g][1][:, col : col + P],
+                        rhs=mq[h][0][:, nh * NH : (nh + 1) * NH].bitcast(FP8X4),
+                        rhs_scale=mq[h][1][:, nh * NH : (nh + 1) * NH],
+                        start=(h == 0),
+                        stop=(h == HALVES - 1),
+                    )
+                nc.scalar.activation(out=bp[:, j, :], in_=pp[:], func=ACT.Copy, scale=tokv[:, g, j : j + 1])
+            ei = work.tile([P, NH, PACK], BF16, name="ei", tag="i4k", bufs=4, align_bytes=64)
+            for q in range(4):
+                bv = psum.tile([P, 512], F32, name="bv", tag="aux")
+                for j in range(PACK):
+                    nc.tensor.matmul(
+                        bv[:, j * P : (j + 1) * P],
+                        lhsT=bdiag[:, g * 4 + j, :],
+                        rhs=val_t[g][:, j, nh * NH + q * P : nh * NH + (q + 1) * P],
+                        start=True,
+                        stop=True,
+                    )
+                nc.vector.tensor_tensor(
+                    out=ei[:, q * P : (q + 1) * P, :].rearrange("p (c i) j -> p c j i", i=RUN),
+                    in0=bv[:].rearrange("p (j c i) -> p c j i", j=PACK, i=RUN),
+                    in1=bp[:, :, q * P : (q + 1) * P].rearrange("p j (c i) -> p c j i", i=RUN),
+                    op=ALU.subtract,
+                )
+            quantize(erq[g], nh * NH, ei[:].rearrange("p n j -> p (n j)"))
+
+        late = {}
+
+        def load_late():
+            for half in range(2):
+                for src, what in ((momentum, "mom"), (memory, "old")):
+                    t = new_raw(what + str(half))
+                    nc.sync.dma_start(
+                        out=t[:],
+                        in_=src[half * 512 : (half + 1) * 512, :].rearrange("(t p) n -> p t n", p=P),
+                    )
+                    late[what, half] = t
+
+        fin = {}
+
+        def finish(c, nh):
+            up = psum.tile([P, NH], F32, name="up", tag="tu", bufs=3)
+            for g in range(GROUPS):
+                nc.tensor.matmul_mx(
+                    out=up[:],
+                    lhsT=kwq[g][0][:, c * P : (c + 1) * P].bitcast(FP8X4),
+                    lhsT_scale=kwq[g][1][:, c * P : (c + 1) * P],
+                    rhs=erq[g][0][:, nh * NH : (nh + 1) * NH].bitcast(FP8X4),
+                    rhs_scale=erq[g][1][:, nh * NH : (nh + 1) * NH],
+                    start=(g == 0),
+                    stop=(g == GROUPS - 1),
+                )
+            cols = slice(nh * NH, (nh + 1) * NH)
+            o1 = work.tile([P, NH], F32, name="o1", tag="o1", bufs=5)
+            nc.vector.scalar_tensor_tensor(
+                out=o1[:],
+                in0=late["mom", c // 4][:, c % 4, cols],
+                scalar=rate_cols[:, c : c + 1],
+                in1=up[:],
+                op0=ALU.mult,
+                op1=ALU.add,
+            )
+            nc.sync.dma_start(out=new_momentum[c * P : (c + 1) * P, cols], in_=o1[:])
+            fin[c, nh] = o1
+
+        def finish_memory(c, nh):
+            cols = slice(nh * NH, (nh + 1) * NH)
+            o1 = fin[c, nh]
+            o0 = work.tile([P, NH], F32, name="o0", tag="o0", bufs=5)
+            if nh == 0:
+                dm = work.tile([P, NH], F32, name="dm", tag="dm", bufs=2)
+                nc.scalar.activation(
+                    out=dm[:], in_=late["old", c // 4][:, c % 4, cols], func=ACT.Copy, scale=rate_cols[:, 8 + c : 9 + c]
+                )
+                nc.gpsimd.tensor_tensor(out=o0[:], in0=dm[:], in1=o1[:], op=ALU.add)
+            else:
+                nc.vector.scalar_tensor_tensor(
+                    out=o0[:],
+                    in0=late["old", c // 4][:, c % 4, cols],
+                    scalar=rate_cols[:, 8 + c : 9 + c],
+                    in1=o1[:],
+                    op0=ALU.mult,
+                    op1=ALU.add,
+                )
+            nc.sync.dma_start(out=new_memory[c * P : (c + 1) * P, cols], in_=o0[:])
+
+        prep(0)
+        mem_quant(0, 0)
+        mem_quant(1, 0)
+        kr(0)
+        prep(1)
+        mem_quant(0, 1)
+        mem_quant(1, 1)
+        val_t.append(load4(values, 1536, "v3"))
+        kw(0)
+        err(0, 0)
+        kr(1)
+        prep(2)
+        kw(1)
+        err(0, 1)
+        err(1, 0)
+        kr(2)
+        prep(3)
+        kw(2)
+        err(1, 1)
+        kr(3)
+        err(2, 0)
+        load_late()
+        kw(3)
+        err(3, 0)
+        for i, g in enumerate(range(EARLY, GROUPS)):
+            for c in range(4 * i, 4 * i + 4):
+                finish(c, 0)
+                finish_memory(c, 0)
+                if c % 4 == 1:
+                    err(g, 1)
+        for c in range(8):
+            finish(c, 1)
+            if c:
+                finish_memory(c - 1, 1)
+        finish_memory(7, 1)

@@ -18,7 +18,6 @@ GROUPS = T // 512
 HALVES = D // 512
 NH = 512
 TABLE_HALVES = (0,)
-POOL_HALVES = (1,)
 EARLY = 2
 RUN = 4
 
@@ -34,19 +33,16 @@ def tile_delta_memory_chunk_f4_kernel(
         raw = ctx.enter_context(tc.tile_pool(name="raw", bufs=7))
         work = ctx.enter_context(tc.tile_pool(name="work", bufs=2))
         stats = ctx.enter_context(tc.tile_pool(name="stats", bufs=4))
-        psc = ctx.enter_context(tc.psum_pool(name="psc", bufs=1))
         psum = ctx.enter_context(tc.psum_pool(name="psum", bufs=2))
 
-        vec_rows = const.tile([P, P], BF16)
+        vec_rows = []
+        for i in range(4):
+            rows = const.tile([P, P], BF16, name="rows%d" % i)
+            nc.vector.memset(rows[:], 0.0)
+            vec_rows.append(rows)
         tok_rows = const.tile([P, 512], BF16)
-        nc.vector.memset(vec_rows[:], 0.0)
         nc.vector.memset(tok_rows[:], 0.0)
         table = const.tile([P, 4, PACK, P], BF16)
-        nc.gpsimd.memset(table[:], 0.0)
-        for i, vec in enumerate((read_gain, write_gain, mu, decay)):
-            nc.scalar.dma_start(out=vec_rows[8 * i : 8 * i + 8, :], in_=vec.rearrange("(r c) -> r c", c=P))
-        nc.scalar.dma_start(out=tok_rows[0:4, :], in_=beta.rearrange("(g c) -> g c", c=512))
-        nc.scalar.dma_start(out=tok_rows[4:8, :], in_=hold.rearrange("(g c) -> g c", c=512))
 
         def new_raw(name):
             t = raw.tile([P, PACK, 1024], BF16, name=name, tag="raw")
@@ -68,12 +64,19 @@ def tile_delta_memory_chunk_f4_kernel(
             )
             mem_t[h, nh] = t
 
+        def load_row(i, vec):
+            nc.sync.dma_start(out=vec_rows[i][0:8, :], in_=vec.rearrange("(r c) -> r c", c=P))
+
         load_k0(0)
         load_k0(1)
+        load_row(0, read_gain)
         load_mem(0, 0)
         load_k0(2)
         load_k0(3)
         load_mem(1, 0)
+        load_row(1, write_gain)
+        nc.sync.dma_start(out=tok_rows[4:8, :], in_=hold.rearrange("(g c) -> g c", c=512))
+        nc.sync.dma_start(out=tok_rows[0:4, :], in_=beta.rearrange("(g c) -> g c", c=512))
         key_t.append(k0)
 
         def load4(src, r0, name):
@@ -89,6 +92,12 @@ def tile_delta_memory_chunk_f4_kernel(
         val_t.append(load4(values, 512, "v1"))
         key_t.append(load4(keys, 1536, "k3"))
         val_t.append(load4(values, 1024, "v2"))
+        load_row(2, mu)
+        load_row(3, decay)
+
+        warm = const.tile([P, 1], F32)
+        nc.vector.memset(warm[:], 0.0)
+        nc.scalar.activation(out=warm[:], in_=warm[:], func=ACT.Square)
 
         ident = const.tile([P, P], BF16)
         make_identity(nc, ident[:])
@@ -97,31 +106,39 @@ def tile_delta_memory_chunk_f4_kernel(
         mhalf = const.tile([P, PACK], F32)
         nc.gpsimd.memset(mhalf[:], -0.5)
 
-        for j in range(PACK):
-            nc.scalar.dma_start(
-                out=table[j : 12 : PACK, :, j, :],
-                in_=write_gain[0:512].rearrange("(o c m) -> o c m", o=1, m=P).to_broadcast([3, 4, P]),
-            )
+        def columns(i, dtype, name):
+            ps = psum.tile([P, P], BF16, name="vec_ps", tag="aux")
+            nc.tensor.transpose(ps[:], vec_rows[i][:], ident[:])
+            cols = const.tile([P, 8], dtype, name=name)
+            nc.scalar.copy(cols[:], ps[:, 0:8])
+            return cols
 
-        vec_ps = psum.tile([P, P], BF16, name="vec_ps", tag="aux")
-        nc.tensor.transpose(vec_ps[:], vec_rows[:], ident[:])
-        gain_cols = const.tile([P, 16], BF16)
-        nc.scalar.copy(gain_cols[:], vec_ps[:, 0:16])
-        rate_cols = const.tile([P, 16], F32)
-        nc.scalar.copy(rate_cols[:], vec_ps[:, 16:32])
+        def spread(cols, count):
+            ps = psum.tile([P, D], BF16, name="row_ps", tag="aux")
+            for r in range(count):
+                nc.tensor.transpose(ps[:, r * P : (r + 1) * P], cols[:, r : r + 1].to_broadcast([P, P]), ident[:])
+            return ps
 
-        rg_ps = psc.tile([P, D], BF16)
-        for r in range(8):
-            nc.tensor.transpose(
-                rg_ps[:, r * P : (r + 1) * P], gain_cols[:, r : r + 1].to_broadcast([P, P]), ident[:]
-            )
-        wg_ps = psum.tile([P, D], BF16, name="wg_ps", tag="aux")
-        for r in range(8):
-            nc.tensor.transpose(
-                wg_ps[:, r * P : (r + 1) * P], gain_cols[:, 8 + r : 9 + r].to_broadcast([P, P]), ident[:]
-            )
-        wgb = const.tile([P, D], BF16)
-        nc.scalar.copy(wgb[:], wg_ps[:])
+        rg_ps = spread(columns(0, BF16, "rg_cols"), 8)
+        rgb = const.tile([P, 2, 256, 2], BF16)
+        nc.scalar.copy(rgb[:], rg_ps[:].rearrange("p (q u e) -> p u q e", u=2, e=2))
+
+        wg_cols = columns(1, BF16, "wg_cols")
+        wg_scale = const.tile([P, 8], F32)
+        nc.scalar.copy(wg_scale[:], wg_cols[:])
+        wg_ps = spread(wg_cols, 4)
+        wgb = const.tile([P, 4, P], BF16)
+        nc.scalar.copy(wgb[:].rearrange("p c m -> p (c m)"), wg_ps[:, 0:512])
+        pick = const.tile([P, PACK], BF16)
+        nc.gpsimd.tensor_tensor(out=pick[:], in0=ident[:, 0:4], in1=ident[:, 4:8], op=ALU.add)
+        pick3 = const.tile([P, PACK], BF16)
+        nc.gpsimd.tensor_tensor(out=pick3[:], in0=pick[:], in1=ident[:, 8:12], op=ALU.add)
+        nc.gpsimd.tensor_tensor(
+            out=table[:],
+            in0=wgb[:].unsqueeze(2).to_broadcast([P, 4, PACK, P]),
+            in1=pick3[:].unsqueeze(1).unsqueeze(3).to_broadcast([P, 4, PACK, P]),
+            op=ALU.mult,
+        )
 
         tok_ps = psum.tile([P, PACK, P], BF16, name="tok_ps", tag="aux")
         for j in range(PACK):
@@ -167,8 +184,21 @@ def tile_delta_memory_chunk_f4_kernel(
         def prep(g):
             ss = stats.tile([P, PACK], F32, name="ss", tag="ss")
             for j in range(PACK):
-                sq = work.tile([P, D], BF16, name="sq", tag="sq", bufs=1)
-                nc.scalar.activation(out=sq[:], in_=key_t[g][:, j, :], func=ACT.Square, accum_out=ss[:, j : j + 1])
+                sq = work.tile([P, D], BF16, name="sq", tag="sq", bufs=2)
+                if g == 0 and j == 0:
+                    nc.vector.scalar_tensor_tensor(
+                        out=sq[:],
+                        in0=key_t[g][:, j, :],
+                        scalar=1.0,
+                        in1=key_t[g][:, j, :],
+                        op0=ALU.mult,
+                        op1=ALU.mult,
+                        accum_out=ss[:, j : j + 1],
+                    )
+                else:
+                    nc.scalar.activation(
+                        out=sq[:], in_=key_t[g][:, j, :], func=ACT.Square, accum_out=ss[:, j : j + 1]
+                    )
             rs = stats.tile([P, PACK], F32, name="rs", tag="rs")
             nc.gpsimd.tensor_tensor(out=rs[:], in0=ss[:], in1=mhalf[:], op=ALU.pow)
             hs = stats.tile([P, PACK], F32, name="hs", tag="hs")
@@ -183,21 +213,22 @@ def tile_delta_memory_chunk_f4_kernel(
                 ki = work.tile([P, 2, 2, P, PACK], BF16, name="ki", tag="i4k", bufs=4, align_bytes=64)
                 for j2 in range(2):
                     j = 2 * jp + j2
-                    kb = work.tile([P, D], BF16, name="kb", tag="kb", bufs=3)
-                    nc.vector.scalar_tensor_tensor(
-                        out=kb[:],
-                        in0=key_t[g][:, j, :],
-                        scalar=rs_t[g][:, j : j + 1],
-                        in1=rg_ps[:],
-                        op0=ALU.mult,
-                        op1=ALU.mult,
-                    )
-                    words = kb[:].bitcast(F32)
-                    tp = psum.tile([P, 2, 2, P], F32, name="tp", tag="tu", bufs=3)
+                    kb = work.tile([P, 2, 256, 2], BF16, name="kb", tag="kb", bufs=3)
+                    for u in range(2):
+                        nc.vector.scalar_tensor_tensor(
+                            out=kb[:, u, :, :],
+                            in0=key_t[g][:, j, :].rearrange("p (q u e) -> p u q e", u=2, e=2)[:, u, :, :],
+                            scalar=rs_t[g][:, j : j + 1],
+                            in1=rgb[:, u, :, :],
+                            op0=ALU.mult,
+                            op1=ALU.mult,
+                        )
+                    words = kb[:].rearrange("p u q e -> p (u q e)").bitcast(F32)
+                    tp = psum.tile([P, 2, 2, P], F32, name="tp", tag="tu", bufs=4)
                     for h in range(2):
                         for u in range(2):
                             nc.tensor.transpose(
-                                tp[:, h, u, :], words[:, 256 * h + u : 256 * (h + 1) : 2], ident_f32[:]
+                                tp[:, h, u, :], words[:, 256 * u + P * h : 256 * u + P * (h + 1)], ident_f32[:]
                             )
                     dst = ki[:].rearrange("p h j m t -> p (h j m t)").bitcast(F32)
                     dst = dst.rearrange("p (h j m u) -> p h j m u", h=2, j=2, u=2)
@@ -235,31 +266,43 @@ def tile_delta_memory_chunk_f4_kernel(
                     )
                 quantize(kwq[g], half * 512, wi[:].rearrange("p n j -> p (n j)"))
 
-        def kw_pool(g):
-            for half in POOL_HALVES:
-                ks = work.tile([P, PACK, NH], F32, name="ks", tag="ks", bufs=1)
-                for j in range(PACK):
+        def kw_turn(g):
+            half = 1
+            ks = work.tile([P, PACK, NH], F32, name="ks", tag="ks", bufs=1)
+            for j in range(PACK):
+                nc.gpsimd.tensor_scalar(
+                    out=ks[:, j, :],
+                    in0=key_t[g][:, j, half * NH : (half + 1) * NH],
+                    scalar1=hs_t[g][:, j : j + 1],
+                    scalar2=0.0,
+                    op0=ALU.mult,
+                    op1=ALU.add,
+                )
+            wi = work.tile([P, NH, PACK], BF16, name="wt", tag="i4k", bufs=4, align_bytes=64)
+            words = wi[:].rearrange("p n j -> p (n j)").bitcast(F32).rearrange("p (c m u) -> p c m u", c=4, u=2)
+            for cp in range(2):
+                back = psum.tile([P, 2, 2, P], F32, name="back", tag="tu", bufs=4)
+                for c2 in range(2):
+                    c = 2 * cp + c2
+                    turn = psum.tile([P, PACK, P], F32, name="turn", tag="tu", bufs=4)
+                    for j in range(PACK):
+                        nc.tensor.transpose(turn[:, j, :], ks[:, j, c * P : (c + 1) * P], ident_f32[:])
+                    kt = work.tile([P, 2, P, 2], BF16, name="kt", tag="kt", bufs=2)
                     nc.scalar.activation(
-                        out=ks[:, j, :],
-                        in_=key_t[g][:, j, half * NH : (half + 1) * NH],
+                        out=kt[:],
+                        in_=turn[:].rearrange("d (u e) m -> d u m e", u=2),
                         func=ACT.Copy,
-                        scale=hs_t[g][:, j : j + 1],
+                        scale=wg_scale[:, half * 4 + c : half * 4 + c + 1],
                     )
-                wi = work.tile([P, NH, PACK], BF16, name="wg", tag="g4k", bufs=2, align_bytes=64)
-                for q in range(4):
-                    cols = slice(q * P, (q + 1) * P)
-                    gains = wgb[:, half * NH + q * P : half * NH + (q + 1) * P]
-                    nc.gpsimd.tensor_tensor(
-                        out=wi[:, cols, :],
-                        in0=ks[:, :, cols].rearrange("p j d -> p d j"),
-                        in1=gains.unsqueeze(2).to_broadcast([P, P, PACK]),
-                        op=ALU.mult,
-                    )
-                quantize(kwq[g], half * 512, wi[:].rearrange("p n j -> p (n j)"))
+                    kt_words = kt[:].rearrange("d u m e -> d (u m e)").bitcast(F32)
+                    for u in range(2):
+                        nc.tensor.transpose(back[:, c2, u, :], kt_words[:, u * P : (u + 1) * P], ident_f32[:])
+                nc.scalar.copy(words[:, 2 * cp : 2 * cp + 2, :, :], back[:].rearrange("p c u m -> p c m u"))
+            quantize(kwq[g], half * 512, wi[:].rearrange("p n j -> p (n j)"))
 
         def kw(g):
             kw_table(g)
-            kw_pool(g)
+            kw_turn(g)
 
         def err(g, nh):
             bp = work.tile([P, PACK, NH], F32, name="bp", tag="bp", bufs=2)
@@ -311,7 +354,7 @@ def tile_delta_memory_chunk_f4_kernel(
         fin = {}
 
         def finish(c, nh):
-            up = psum.tile([P, NH], F32, name="up", tag="tu", bufs=3)
+            up = psum.tile([P, NH], F32, name="up", tag="tu", bufs=4)
             for g in range(GROUPS):
                 nc.tensor.matmul_mx(
                     out=up[:],
@@ -327,7 +370,7 @@ def tile_delta_memory_chunk_f4_kernel(
             nc.vector.scalar_tensor_tensor(
                 out=o1[:],
                 in0=late["mom", c // 4][:, c % 4, cols],
-                scalar=rate_cols[:, c : c + 1],
+                scalar=mu_cols[:, c : c + 1],
                 in1=up[:],
                 op0=ALU.mult,
                 op1=ALU.add,
@@ -335,24 +378,18 @@ def tile_delta_memory_chunk_f4_kernel(
             nc.sync.dma_start(out=new_momentum[c * P : (c + 1) * P, cols], in_=o1[:])
             fin[c, nh] = o1
 
-        def finish_memory(c, nh):
+        def finish_memory(c, nh, pool):
             cols = slice(nh * NH, (nh + 1) * NH)
             o1 = fin[c, nh]
             o0 = work.tile([P, NH], F32, name="o0", tag="o0", bufs=5)
-            if nh == 0:
-                dm = work.tile([P, NH], F32, name="dm", tag="dm", bufs=2)
-                nc.scalar.activation(
-                    out=dm[:], in_=late["old", c // 4][:, c % 4, cols], func=ACT.Copy, scale=rate_cols[:, 8 + c : 9 + c]
-                )
+            old = late["old", c // 4][:, c % 4, cols]
+            if pool:
+                dm = work.tile([P, NH], F32, name="dm", tag="dm", bufs=3)
+                nc.scalar.activation(out=dm[:], in_=old, func=ACT.Copy, scale=decay_cols[:, c : c + 1])
                 nc.gpsimd.tensor_tensor(out=o0[:], in0=dm[:], in1=o1[:], op=ALU.add)
             else:
                 nc.vector.scalar_tensor_tensor(
-                    out=o0[:],
-                    in0=late["old", c // 4][:, c % 4, cols],
-                    scalar=rate_cols[:, 8 + c : 9 + c],
-                    in1=o1[:],
-                    op0=ALU.mult,
-                    op1=ALU.add,
+                    out=o0[:], in0=old, scalar=decay_cols[:, c : c + 1], in1=o1[:], op0=ALU.mult, op1=ALU.add
                 )
             nc.sync.dma_start(out=new_memory[c * P : (c + 1) * P, cols], in_=o0[:])
 
@@ -378,16 +415,18 @@ def tile_delta_memory_chunk_f4_kernel(
         kr(3)
         err(2, 0)
         load_late()
+        mu_cols = columns(2, F32, "mu_cols")
+        decay_cols = columns(3, F32, "decay_cols")
         kw(3)
         err(3, 0)
         for i, g in enumerate(range(EARLY, GROUPS)):
             for c in range(4 * i, 4 * i + 4):
                 finish(c, 0)
-                finish_memory(c, 0)
+                finish_memory(c, 0, True)
                 if c % 4 == 1:
                     err(g, 1)
         for c in range(8):
             finish(c, 1)
             if c:
-                finish_memory(c - 1, 1)
-        finish_memory(7, 1)
+                finish_memory(c - 1, 1, c % 2 == 1)
+        finish_memory(7, 1, False)

@@ -17,7 +17,6 @@ PACK = 4
 GROUPS = T // 512
 HALVES = D // 512
 NH = 512
-TABLE_HALVES = (0,)
 EARLY = 2
 RUN = 4
 
@@ -42,7 +41,6 @@ def tile_delta_memory_chunk_f4_kernel(
             vec_rows.append(rows)
         tok_rows = const.tile([P, 512], BF16)
         nc.vector.memset(tok_rows[:], 0.0)
-        table = const.tile([P, 4, PACK, P], BF16)
 
         def new_raw(name):
             t = raw.tile([P, PACK, 1024], BF16, name=name, tag="raw")
@@ -120,25 +118,13 @@ def tile_delta_memory_chunk_f4_kernel(
             return ps
 
         rg_ps = spread(columns(0, BF16, "rg_cols"), 8)
-        rgb = const.tile([P, 2, 256, 2], BF16)
-        nc.scalar.copy(rgb[:], rg_ps[:].rearrange("p (q u e) -> p u q e", u=2, e=2))
+        rgb = const.tile([P, D], BF16)
+        nc.scalar.copy(rgb[:], rg_ps[:])
 
         wg_cols = columns(1, BF16, "wg_cols")
-        wg_scale = const.tile([P, 8], F32)
-        nc.scalar.copy(wg_scale[:], wg_cols[:])
-        wg_ps = spread(wg_cols, 4)
-        wgb = const.tile([P, 4, P], BF16)
-        nc.scalar.copy(wgb[:].rearrange("p c m -> p (c m)"), wg_ps[:, 0:512])
-        pick = const.tile([P, PACK], BF16)
-        nc.gpsimd.tensor_tensor(out=pick[:], in0=ident[:, 0:4], in1=ident[:, 4:8], op=ALU.add)
-        pick3 = const.tile([P, PACK], BF16)
-        nc.gpsimd.tensor_tensor(out=pick3[:], in0=pick[:], in1=ident[:, 8:12], op=ALU.add)
-        nc.gpsimd.tensor_tensor(
-            out=table[:],
-            in0=wgb[:].unsqueeze(2).to_broadcast([P, 4, PACK, P]),
-            in1=pick3[:].unsqueeze(1).unsqueeze(3).to_broadcast([P, 4, PACK, P]),
-            op=ALU.mult,
-        )
+        wg_ps = spread(wg_cols, 8)
+        wgb = const.tile([P, D], BF16)
+        nc.scalar.copy(wgb[:], wg_ps[:])
 
         tok_ps = psum.tile([P, PACK, P], BF16, name="tok_ps", tag="aux")
         for j in range(PACK):
@@ -171,7 +157,7 @@ def tile_delta_memory_chunk_f4_kernel(
             )
 
         def mem_quant(h, nh):
-            mi = work.tile([P, NH, PACK], BF16, name="mi", tag="i4k", bufs=4, align_bytes=64)
+            mi = work.tile([P, NH, PACK], BF16, name="mi", tag="i4k", bufs=3, align_bytes=64)
             src = mem_t[h, nh][:]
             nc.vector.tensor_copy(
                 out=mi[:].rearrange("p (c i) j -> p c j i", i=RUN),
@@ -206,106 +192,56 @@ def tile_delta_memory_chunk_f4_kernel(
             rs_t[g], hs_t[g] = rs, hs
 
         def kr(g):
-            codes = raw.tile([P, 1024], U32, name="krq_c%d" % g, tag="krq_c", bufs=3, align_bytes=64)
-            scales = raw.tile([P, 1024], U8, name="krq_s%d" % g, tag="krq_s", bufs=3, align_bytes=64)
+            codes = raw.tile([P, 1024], U32, name="krq_c%d" % g, tag="krq_c", bufs=2, align_bytes=64)
+            scales = raw.tile([P, 1024], U8, name="krq_s%d" % g, tag="krq_s", bufs=2, align_bytes=64)
             krq[g] = (codes, scales)
+            ki = work.tile([P, 2, 2, 2, P, PACK], BF16, name="ki", tag="i8k", bufs=2, align_bytes=64)
             for jp in range(2):
-                ki = work.tile([P, 2, 2, P, PACK], BF16, name="ki", tag="i4k", bufs=4, align_bytes=64)
                 for j2 in range(2):
                     j = 2 * jp + j2
-                    kb = work.tile([P, 2, 256, 2], BF16, name="kb", tag="kb", bufs=3)
-                    for u in range(2):
-                        nc.vector.scalar_tensor_tensor(
-                            out=kb[:, u, :, :],
-                            in0=key_t[g][:, j, :].rearrange("p (q u e) -> p u q e", u=2, e=2)[:, u, :, :],
-                            scalar=rs_t[g][:, j : j + 1],
-                            in1=rgb[:, u, :, :],
-                            op0=ALU.mult,
-                            op1=ALU.mult,
-                        )
-                    words = kb[:].rearrange("p u q e -> p (u q e)").bitcast(F32)
+                    kb = work.tile([P, D], BF16, name="kb", tag="kb", bufs=2)
+                    nc.vector.scalar_tensor_tensor(
+                        out=kb[:],
+                        in0=key_t[g][:, j, :],
+                        scalar=rs_t[g][:, j : j + 1],
+                        in1=rgb[:],
+                        op0=ALU.mult,
+                        op1=ALU.mult,
+                    )
+                    words = kb[:].bitcast(F32)
                     tp = psum.tile([P, 2, 2, P], F32, name="tp", tag="tu", bufs=4)
                     for h in range(2):
                         for u in range(2):
                             nc.tensor.transpose(
-                                tp[:, h, u, :], words[:, 256 * u + P * h : 256 * u + P * (h + 1)], ident_f32[:]
+                                tp[:, h, u, :], words[:, 256 * h + u : 256 * (h + 1) : 2], ident_f32[:]
                             )
-                    dst = ki[:].rearrange("p h j m t -> p (h j m t)").bitcast(F32)
-                    dst = dst.rearrange("p (h j m u) -> p h j m u", h=2, j=2, u=2)
-                    nc.scalar.copy(dst[:, :, j2, :, :], tp[:].rearrange("p h u m -> p h m u"))
-                quantize(krq[g], 512 * jp, ki[:].rearrange("p h j m t -> p (h j m t)"))
-
-        def kw_table(g):
-            st = stats.tile([P, P], BF16, name="st%d" % g, tag="st%d" % g, bufs=1)
-            nc.gpsimd.memset(st[:], 0.0)
-            hs = hs_t[g]
-            r1 = stats.tile([P, PACK], F32, name="r1", tag="r1", bufs=2)
-            r2 = stats.tile([P, PACK], F32, name="r2", tag="r2", bufs=2)
-            nc.gpsimd.tensor_copy(out=st[:, 0:4], in_=hs[:])
-            nc.gpsimd.tensor_tensor(out=r1[:], in0=hs[:], in1=st[:, 0:4], op=ALU.subtract)
-            nc.gpsimd.tensor_copy(out=st[:, 4:8], in_=r1[:])
-            nc.gpsimd.tensor_tensor(out=r2[:], in0=r1[:], in1=st[:, 4:8], op=ALU.subtract)
-            nc.gpsimd.tensor_copy(out=st[:, 8:12], in_=r2[:])
-            hp = psum.tile([P, P], BF16, name="hp", tag="aux")
-            nc.tensor.transpose(hp[:], st[:], ident[:])
-            ht = stats.tile([P, P], BF16, name="ht", tag="ht", bufs=2)
-            nc.scalar.copy(ht[:], hp[:])
-            for half in TABLE_HALVES:
-                wi = work.tile([P, NH, PACK], BF16, name="wi", tag="i4k", bufs=4, align_bytes=64)
-                for q in range(4):
-                    c = 4 * half + q
-                    fb = psum.tile([P, 512], F32, name="fb", tag="aux")
-                    nc.tensor.matmul(
-                        fb[:], lhsT=ht[:], rhs=table[:, c, :, :].rearrange("p j m -> p (j m)"), start=True, stop=True
-                    )
-                    nc.vector.tensor_tensor(
-                        out=wi[:, q * P : (q + 1) * P, :].rearrange("p (c i) j -> p c j i", i=RUN),
-                        in0=key_t[g][:, :, c * P : (c + 1) * P].rearrange("p j (c i) -> p c j i", i=RUN),
-                        in1=fb[:].rearrange("p (j c i) -> p c j i", j=PACK, i=RUN),
-                        op=ALU.mult,
-                    )
-                quantize(kwq[g], half * 512, wi[:].rearrange("p n j -> p (n j)"))
-
-        def kw_turn(g):
-            half = 1
-            ks = work.tile([P, PACK, NH], F32, name="ks", tag="ks", bufs=1)
-            for j in range(PACK):
-                nc.gpsimd.tensor_scalar(
-                    out=ks[:, j, :],
-                    in0=key_t[g][:, j, half * NH : (half + 1) * NH],
-                    scalar1=hs_t[g][:, j : j + 1],
-                    scalar2=0.0,
-                    op0=ALU.mult,
-                    op1=ALU.add,
-                )
-            wi = work.tile([P, NH, PACK], BF16, name="wt", tag="i4k", bufs=4, align_bytes=64)
-            words = wi[:].rearrange("p n j -> p (n j)").bitcast(F32).rearrange("p (c m u) -> p c m u", c=4, u=2)
-            for cp in range(2):
-                back = psum.tile([P, 2, 2, P], F32, name="back", tag="tu", bufs=4)
-                for c2 in range(2):
-                    c = 2 * cp + c2
-                    turn = psum.tile([P, PACK, P], F32, name="turn", tag="tu", bufs=4)
-                    for j in range(PACK):
-                        nc.tensor.transpose(turn[:, j, :], ks[:, j, c * P : (c + 1) * P], ident_f32[:])
-                    kt = work.tile([P, 2, P, 2], BF16, name="kt", tag="kt", bufs=2)
-                    nc.scalar.activation(
-                        out=kt[:],
-                        in_=turn[:].rearrange("d (u e) m -> d u m e", u=2),
-                        func=ACT.Copy,
-                        scale=wg_scale[:, half * 4 + c : half * 4 + c + 1],
-                    )
-                    kt_words = kt[:].rearrange("d u m e -> d (u m e)").bitcast(F32)
-                    for u in range(2):
-                        nc.tensor.transpose(back[:, c2, u, :], kt_words[:, u * P : (u + 1) * P], ident_f32[:])
-                nc.scalar.copy(words[:, 2 * cp : 2 * cp + 2, :, :], back[:].rearrange("p c u m -> p c m u"))
-            quantize(kwq[g], half * 512, wi[:].rearrange("p n j -> p (n j)"))
+                    dst = ki[:].rearrange("p q h j m t -> p (q h j m t)").bitcast(F32)
+                    dst = dst.rearrange("p (q h j m u) -> p q h j m u", q=2, h=2, j=2, u=2)
+                    nc.scalar.copy(dst[:, jp, :, j2, :, :], tp[:].rearrange("p h u m -> p h m u"))
+            quantize(krq[g], 0, ki[:].rearrange("p q h j m t -> p (q h j m t)"))
 
         def kw(g):
-            kw_table(g)
-            kw_turn(g)
+            wi = work.tile([P, D, PACK], BF16, name="wi", tag="i8k", bufs=2, align_bytes=64)
+            for half in range(2):
+                cols = slice(half * NH, (half + 1) * NH)
+                ks = work.tile([P, PACK, NH], F32, name="ks", tag="f8k", bufs=4)
+                for j in range(PACK):
+                    nc.scalar.activation(
+                        out=ks[:, j, :], in_=key_t[g][:, j, cols], func=ACT.Copy, scale=hs_t[g][:, j : j + 1]
+                    )
+                nc.vector.tensor_tensor(
+                    out=wi[:, cols, :].rearrange("p (c i) j -> p c j i", i=RUN),
+                    in0=ks[:].rearrange("p j (c i) -> p c j i", i=RUN),
+                    in1=wgb[:, cols]
+                    .rearrange("p (c i) -> p c i", i=RUN)
+                    .unsqueeze(2)
+                    .to_broadcast([P, NH // RUN, PACK, RUN]),
+                    op=ALU.mult,
+                )
+            quantize(kwq[g], 0, wi[:].rearrange("p n j -> p (n j)"))
 
         def err(g, nh):
-            bp = work.tile([P, PACK, NH], F32, name="bp", tag="bp", bufs=2)
+            bp = work.tile([P, PACK, NH], F32, name="bp", tag="f8k", bufs=4)
             for j in range(PACK):
                 pp = psum.tile([P, NH], F32, name="pp", tag="pp")
                 for h in range(HALVES):
@@ -320,7 +256,24 @@ def tile_delta_memory_chunk_f4_kernel(
                         stop=(h == HALVES - 1),
                     )
                 nc.scalar.activation(out=bp[:, j, :], in_=pp[:], func=ACT.Copy, scale=tokv[:, g, j : j + 1])
-            ei = work.tile([P, NH, PACK], BF16, name="ei", tag="i4k", bufs=4, align_bytes=64)
+            ei = work.tile([P, NH, PACK], BF16, name="ei", tag="i4k", bufs=3, align_bytes=64)
+            if nh == 1 and g >= EARLY:
+                bs = work.tile([P, PACK, NH], F32, name="bs", tag="f8k", bufs=4)
+                for j in range(PACK):
+                    nc.scalar.activation(
+                        out=bs[:, j, :],
+                        in_=val_t[g][:, j, nh * NH : (nh + 1) * NH],
+                        func=ACT.Copy,
+                        scale=tokv[:, g, j : j + 1],
+                    )
+                nc.vector.tensor_tensor(
+                    out=ei[:].rearrange("p (c i) j -> p c j i", i=RUN),
+                    in0=bs[:].rearrange("p j (c i) -> p c j i", i=RUN),
+                    in1=bp[:].rearrange("p j (c i) -> p c j i", i=RUN),
+                    op=ALU.subtract,
+                )
+                quantize(erq[g], nh * NH, ei[:].rearrange("p n j -> p (n j)"))
+                return
             for q in range(4):
                 bv = psum.tile([P, 512], F32, name="bv", tag="aux")
                 for j in range(PACK):
@@ -366,7 +319,7 @@ def tile_delta_memory_chunk_f4_kernel(
                     stop=(g == GROUPS - 1),
                 )
             cols = slice(nh * NH, (nh + 1) * NH)
-            o1 = work.tile([P, NH], F32, name="o1", tag="o1", bufs=5)
+            o1 = work.tile([P, NH], F32, name="o1", tag="o1", bufs=4)
             nc.vector.scalar_tensor_tensor(
                 out=o1[:],
                 in0=late["mom", c // 4][:, c % 4, cols],
@@ -381,7 +334,7 @@ def tile_delta_memory_chunk_f4_kernel(
         def finish_memory(c, nh, pool):
             cols = slice(nh * NH, (nh + 1) * NH)
             o1 = fin[c, nh]
-            o0 = work.tile([P, NH], F32, name="o0", tag="o0", bufs=5)
+            o0 = work.tile([P, NH], F32, name="o0", tag="o0", bufs=4)
             old = late["old", c // 4][:, c % 4, cols]
             if pool:
                 dm = work.tile([P, NH], F32, name="dm", tag="dm", bufs=3)

from contextlib import ExitStack

import concourse.mybir as mybir
from concourse.masks import make_identity

F32 = mybir.dt.float32
BF16 = mybir.dt.bfloat16
U32 = mybir.dt.uint32
U8 = mybir.dt.uint8
FP8X4 = mybir.dt.float8_e4m3fn_x4
ACT = mybir.ActivationFunctionType
ALU = mybir.AluOpType

P = 128
T, D, N = 2048, 1024, 1024
PACK = 4
GROUPS = T // 512
HALVES = D // 512
NH = 512
EARLY = 2
RUN = 4

FLOPS = 2 * 2 * T * D * N


def tile_delta_memory_chunk_f4_kernel(
    tc, keys, values, memory, momentum, read_gain, write_gain, beta, hold, decay, mu, new_memory, new_momentum
):
    nc = tc.nc
    with ExitStack() as ctx:
        const = ctx.enter_context(tc.tile_pool(name="const", bufs=1))
        raw = ctx.enter_context(tc.tile_pool(name="raw", bufs=7))
        work = ctx.enter_context(tc.tile_pool(name="work", bufs=2))
        stats = ctx.enter_context(tc.tile_pool(name="stats", bufs=4))
        psum = ctx.enter_context(tc.psum_pool(name="psum", bufs=2))

        vec_rows = []
        for i in range(4):
            rows = const.tile([P, P], BF16, name="rows%d" % i)
            nc.vector.memset(rows[:], 0.0)
            vec_rows.append(rows)
        tok_rows = const.tile([P, 512], BF16)
        nc.vector.memset(tok_rows[:], 0.0)

        def new_raw(name):
            t = raw.tile([P, PACK, 1024], BF16, name=name, tag="raw")
            return t

        key_t, val_t, mem_t = [], [], {}
        k0 = new_raw("k0")

        def load_k0(j):
            nc.sync.dma_start(
                out=k0[:, j, :], in_=keys[0:512, :].rearrange("(p j) d -> p j d", j=PACK)[:, j, :]
            )

        def load_mem(h, nh):
            cols = slice(nh * NH, (nh + 1) * NH)
            t = raw.tile([P, PACK, NH], BF16, name="m%d%d" % (h, nh), tag="mraw", bufs=4)
            nc.sync.dma_start(
                out=t[:], in_=memory[h * 512 : (h + 1) * 512, cols].rearrange("(p j) n -> p j n", j=PACK)
            )
            mem_t[h, nh] = t

        def load_row(i, vec):
            nc.sync.dma_start(out=vec_rows[i][0:8, :], in_=vec.rearrange("(r c) -> r c", c=P))

        load_k0(0)
        load_k0(1)
        load_row(0, read_gain)
        load_mem(0, 0)
        load_k0(2)
        load_k0(3)
        load_mem(1, 0)
        load_row(1, write_gain)
        nc.sync.dma_start(out=tok_rows[4:8, :], in_=hold.rearrange("(g c) -> g c", c=512))
        nc.sync.dma_start(out=tok_rows[0:4, :], in_=beta.rearrange("(g c) -> g c", c=512))
        key_t.append(k0)

        def load4(src, r0, name):
            t = new_raw(name)
            nc.sync.dma_start(out=t[:], in_=src[r0 : r0 + 512, :].rearrange("(p j) d -> p j d", j=PACK))
            return t

        key_t.append(load4(keys, 512, "k1"))
        load_mem(0, 1)
        load_mem(1, 1)
        val_t.append(load4(values, 0, "v0"))
        key_t.append(load4(keys, 1024, "k2"))
        val_t.append(load4(values, 512, "v1"))
        key_t.append(load4(keys, 1536, "k3"))
        val_t.append(load4(values, 1024, "v2"))
        load_row(2, mu)
        load_row(3, decay)

        warm = const.tile([P, 1], F32)
        nc.vector.memset(warm[:], 0.0)
        nc.scalar.activation(out=warm[:], in_=warm[:], func=ACT.Square)

        ident = const.tile([P, P], BF16)
        make_identity(nc, ident[:])
        ident_f32 = const.tile([P, P], F32)
        make_identity(nc, ident_f32[:])
        mhalf = const.tile([P, PACK], F32)
        nc.gpsimd.memset(mhalf[:], -0.5)

        def columns(i, dtype, name):
            ps = psum.tile([P, P], BF16, name="vec_ps", tag="aux")
            nc.tensor.transpose(ps[:], vec_rows[i][:], ident[:])
            cols = const.tile([P, 8], dtype, name=name)
            nc.scalar.copy(cols[:], ps[:, 0:8])
            return cols

        def spread(cols, count):
            ps = psum.tile([P, D], BF16, name="row_ps", tag="aux")
            for r in range(count):
                nc.tensor.transpose(ps[:, r * P : (r + 1) * P], cols[:, r : r + 1].to_broadcast([P, P]), ident[:])
            return ps

        rg_ps = spread(columns(0, BF16, "rg_cols"), 8)
        rgb = const.tile([P, D], BF16)
        nc.scalar.copy(rgb[:], rg_ps[:])

        wg_cols = columns(1, BF16, "wg_cols")
        wg_ps = spread(wg_cols, 8)
        wgb = const.tile([P, D], BF16)
        nc.scalar.copy(wgb[:], wg_ps[:])

        tok_ps = psum.tile([P, PACK, P], BF16, name="tok_ps", tag="aux")
        for j in range(PACK):
            nc.tensor.transpose(tok_ps[:, j, :], tok_rows[:, j:512:PACK], ident[:])
        tokv = const.tile([P, 8, PACK], F32)
        nc.scalar.copy(tokv[:], tok_ps[:, :, 0:8].rearrange("p j k -> p k j"))

        bdiag = const.tile([P, 16, P], BF16)
        nc.gpsimd.tensor_tensor(
            out=bdiag[:],
            in0=ident[:].unsqueeze(1).to_broadcast([P, 16, P]),
            in1=tokv[:, 0:4, :].rearrange("p g j -> p (g j)").unsqueeze(2).to_broadcast([P, 16, P]),
            op=ALU.mult,
        )

        def plane(name, cols):
            codes = const.tile([P, cols], U32, name=name + "_c", align_bytes=64)
            scales = const.tile([P, cols], U8, name=name + "_s", align_bytes=64)
            return codes, scales

        mq = [plane("mq0", N), plane("mq1", N)]
        krq = {}
        kwq = [plane("kwq0", D), plane("kwq1", D), plane("kwq2", D), plane("kwq3", D)]
        erq = [plane("erq0", N), plane("erq1", N), plane("erq2", N), plane("erq3", N)]

        def quantize(dst, c0, src):
            width = src.shape[-1] // PACK
            nc.vector.quantize_mx(
                out=dst[0][:, c0 : c0 + width].bitcast(FP8X4), scales=dst[1][:, c0 : c0 + width], in_=src
            )

        def mem_quant(h, nh):
            mi = work.tile([P, NH, PACK], BF16, name="mi", tag="i4k", bufs=3, align_bytes=64)
            src = mem_t[h, nh][:]
            nc.vector.tensor_copy(
                out=mi[:].rearrange("p (c i) j -> p c j i", i=RUN),
                in_=src.rearrange("p j (c i) -> p c j i", i=RUN),
            )
            quantize(mq[h], nh * NH, mi[:].rearrange("p n j -> p (n j)"))

        rs_t, hs_t = {}, {}

        def prep(g):
            ss = stats.tile([P, PACK], F32, name="ss", tag="ss")
            for j in range(PACK):
                sq = work.tile([P, D], BF16, name="sq", tag="sq", bufs=2)
                if g == 0 and j == 0:
                    nc.vector.scalar_tensor_tensor(
                        out=sq[:],
                        in0=key_t[g][:, j, :],
                        scalar=1.0,
                        in1=key_t[g][:, j, :],
                        op0=ALU.mult,
                        op1=ALU.mult,
                        accum_out=ss[:, j : j + 1],
                    )
                else:
                    nc.scalar.activation(
                        out=sq[:], in_=key_t[g][:, j, :], func=ACT.Square, accum_out=ss[:, j : j + 1]
                    )
            rs = stats.tile([P, PACK], F32, name="rs", tag="rs")
            nc.gpsimd.tensor_tensor(out=rs[:], in0=ss[:], in1=mhalf[:], op=ALU.pow)
            hs = stats.tile([P, PACK], F32, name="hs", tag="hs")
            nc.gpsimd.tensor_tensor(out=hs[:], in0=rs[:], in1=tokv[:, 4 + g, :], op=ALU.mult)
            rs_t[g], hs_t[g] = rs, hs

        def kr(g):
            codes = raw.tile([P, 1024], U32, name="krq_c%d" % g, tag="krq_c", bufs=2, align_bytes=64)
            scales = raw.tile([P, 1024], U8, name="krq_s%d" % g, tag="krq_s", bufs=2, align_bytes=64)
            krq[g] = (codes, scales)
            ki = work.tile([P, 2, 2, 2, P, PACK], BF16, name="ki", tag="i8k", bufs=2, align_bytes=64)
            for jp in range(2):
                for j2 in range(2):
                    j = 2 * jp + j2
                    kb = work.tile([P, D], BF16, name="kb", tag="kb", bufs=2)
                    nc.vector.scalar_tensor_tensor(
                        out=kb[:],
                        in0=key_t[g][:, j, :],
                        scalar=rs_t[g][:, j : j + 1],
                        in1=rgb[:],
                        op0=ALU.mult,
                        op1=ALU.mult,
                    )
                    words = kb[:].bitcast(F32)
                    tp = psum.tile([P, 2, 2, P], F32, name="tp", tag="tu", bufs=4)
                    for h in range(2):
                        for u in range(2):
                            nc.tensor.transpose(
                                tp[:, h, u, :], words[:, 256 * h + u : 256 * (h + 1) : 2], ident_f32[:]
                            )
                    dst = ki[:].rearrange("p q h j m t -> p (q h j m t)").bitcast(F32)
                    dst = dst.rearrange("p (q h j m u) -> p q h j m u", q=2, h=2, j=2, u=2)
                    nc.scalar.copy(dst[:, jp, :, j2, :, :], tp[:].rearrange("p h u m -> p h m u"))
            quantize(krq[g], 0, ki[:].rearrange("p q h j m t -> p (q h j m t)"))

        def kw(g):
            wi = work.tile([P, D, PACK], BF16, name="wi", tag="i8k", bufs=2, align_bytes=64)
            for half in range(2):
                cols = slice(half * NH, (half + 1) * NH)
                ks = work.tile([P, PACK, NH], F32, name="ks", tag="f8k", bufs=4)
                for j in range(PACK):
                    nc.scalar.activation(
                        out=ks[:, j, :], in_=key_t[g][:, j, cols], func=ACT.Copy, scale=hs_t[g][:, j : j + 1]
                    )
                nc.vector.tensor_tensor(
                    out=wi[:, cols, :].rearrange("p (c i) j -> p c j i", i=RUN),
                    in0=ks[:].rearrange("p j (c i) -> p c j i", i=RUN),
                    in1=wgb[:, cols]
                    .rearrange("p (c i) -> p c i", i=RUN)
                    .unsqueeze(2)
                    .to_broadcast([P, NH // RUN, PACK, RUN]),
                    op=ALU.mult,
                )
            quantize(kwq[g], 0, wi[:].rearrange("p n j -> p (n j)"))

        def err(g, nh):
            bp = work.tile([P, PACK, NH], F32, name="bp", tag="f8k", bufs=4)
            for j in range(PACK):
                pp = psum.tile([P, NH], F32, name="pp", tag="pp")
                for h in range(HALVES):
                    col = (((j // 2) * 2 + h) * 2 + j % 2) * P
                    nc.tensor.matmul_mx(
                        out=pp[:],
                        lhsT=krq[g][0][:, col : col + P].bitcast(FP8X4),
                        lhsT_scale=krq[g][1][:, col : col + P],
                        rhs=mq[h][0][:, nh * NH : (nh + 1) * NH].bitcast(FP8X4),
                        rhs_scale=mq[h][1][:, nh * NH : (nh + 1) * NH],
                        start=(h == 0),
                        stop=(h == HALVES - 1),
                    )
                nc.scalar.activation(out=bp[:, j, :], in_=pp[:], func=ACT.Copy, scale=tokv[:, g, j : j + 1])
            ei = work.tile([P, NH, PACK], BF16, name="ei", tag="i4k", bufs=3, align_bytes=64)
            if nh == 1 and g >= EARLY:
                bs = work.tile([P, PACK, NH], F32, name="bs", tag="f8k", bufs=4)
                for j in range(PACK):
                    nc.scalar.activation(
                        out=bs[:, j, :],
                        in_=val_t[g][:, j, nh * NH : (nh + 1) * NH],
                        func=ACT.Copy,
                        scale=tokv[:, g, j : j + 1],
                    )
                nc.vector.tensor_tensor(
                    out=ei[:].rearrange("p (c i) j -> p c j i", i=RUN),
                    in0=bs[:].rearrange("p j (c i) -> p c j i", i=RUN),
                    in1=bp[:].rearrange("p j (c i) -> p c j i", i=RUN),
                    op=ALU.subtract,
                )
                quantize(erq[g], nh * NH, ei[:].rearrange("p n j -> p (n j)"))
                return
            for q in range(4):
                bv = psum.tile([P, 512], F32, name="bv", tag="aux")
                for j in range(PACK):
                    nc.tensor.matmul(
                        bv[:, j * P : (j + 1) * P],
                        lhsT=bdiag[:, g * 4 + j, :],
                        rhs=val_t[g][:, j, nh * NH + q * P : nh * NH + (q + 1) * P],
                        start=True,
                        stop=True,
                    )
                nc.vector.tensor_tensor(
                    out=ei[:, q * P : (q + 1) * P, :].rearrange("p (c i) j -> p c j i", i=RUN),
                    in0=bv[:].rearrange("p (j c i) -> p c j i", j=PACK, i=RUN),
                    in1=bp[:, :, q * P : (q + 1) * P].rearrange("p j (c i) -> p c j i", i=RUN),
                    op=ALU.subtract,
                )
            quantize(erq[g], nh * NH, ei[:].rearrange("p n j -> p (n j)"))

        late = {}

        def load_late():
            for half in range(2):
                for src, what in ((momentum, "mom"), (memory, "old")):
                    t = new_raw(what + str(half))
                    nc.sync.dma_start(
                        out=t[:],
                        in_=src[half * 512 : (half + 1) * 512, :].rearrange("(t p) n -> p t n", p=P),
                    )
                    late[what, half] = t

        fin = {}

        def finish(c, nh):
            up = psum.tile([P, NH], F32, name="up", tag="tu", bufs=4)
            for g in range(GROUPS):
                nc.tensor.matmul_mx(
                    out=up[:],
                    lhsT=kwq[g][0][:, c * P : (c + 1) * P].bitcast(FP8X4),
                    lhsT_scale=kwq[g][1][:, c * P : (c + 1) * P],
                    rhs=erq[g][0][:, nh * NH : (nh + 1) * NH].bitcast(FP8X4),
                    rhs_scale=erq[g][1][:, nh * NH : (nh + 1) * NH],
                    start=(g == 0),
                    stop=(g == GROUPS - 1),
                )
            cols = slice(nh * NH, (nh + 1) * NH)
            o1 = work.tile([P, NH], F32, name="o1", tag="o1", bufs=4)
            nc.vector.scalar_tensor_tensor(
                out=o1[:],
                in0=late["mom", c // 4][:, c % 4, cols],
                scalar=mu_cols[:, c : c + 1],
                in1=up[:],
                op0=ALU.mult,
                op1=ALU.add,
            )
            nc.sync.dma_start(out=new_momentum[c * P : (c + 1) * P, cols], in_=o1[:])
            fin[c, nh] = o1

        def finish_memory(c, nh, pool):
            cols = slice(nh * NH, (nh + 1) * NH)
            o1 = fin[c, nh]
            o0 = work.tile([P, NH], F32, name="o0", tag="o0", bufs=4)
            old = late["old", c // 4][:, c % 4, cols]
            if pool:
                dm = work.tile([P, NH], F32, name="dm", tag="dm", bufs=3)
                nc.scalar.activation(out=dm[:], in_=old, func=ACT.Copy, scale=decay_cols[:, c : c + 1])
                nc.gpsimd.tensor_tensor(out=o0[:], in0=dm[:], in1=o1[:], op=ALU.add)
            else:
                nc.vector.scalar_tensor_tensor(
                    out=o0[:], in0=old, scalar=decay_cols[:, c : c + 1], in1=o1[:], op0=ALU.mult, op1=ALU.add
                )
            nc.sync.dma_start(out=new_memory[c * P : (c + 1) * P, cols], in_=o0[:])

        prep(0)
        mem_quant(0, 0)
        mem_quant(1, 0)
        kr(0)
        prep(1)
        mem_quant(0, 1)
        mem_quant(1, 1)
        val_t.append(load4(values, 1536, "v3"))
        kw(0)
        err(0, 0)
        kr(1)
        prep(2)
        kw(1)
        err(0, 1)
        err(1, 0)
        kr(2)
        prep(3)
        kw(2)
        err(1, 1)
        kr(3)
        err(2, 0)
        load_late()
        mu_cols = columns(2, F32, "mu_cols")
        decay_cols = columns(3, F32, "decay_cols")
        kw(3)
        err(3, 0)
        for i, g in enumerate(range(EARLY, GROUPS)):
            for c in range(4 * i, 4 * i + 4):
                finish(c, 0)
                finish_memory(c, 0, True)
                if c % 4 == 1:
                    err(g, 1)
        for c in range(8):
            finish(c, 1)
            if c:
                finish_memory(c - 1, 1, c % 2 == 1)
        finish_memory(7, 1, False)
